import numpy as np
import ml_dtypes


def mxq(x, axis, fmt="e4m3"):
    dtype, down = {"e4m3": (ml_dtypes.float8_e4m3fn, 7), "e5m2": (ml_dtypes.float8_e5m2, 14)}[fmt]
    v = np.moveaxis(np.asarray(x, np.float32).astype(ml_dtypes.bfloat16).astype(np.float64), axis, -1)
    blocks = v.reshape(v.shape[:-1] + (-1, 32))
    amax = np.abs(blocks).max(-1, keepdims=True)
    byte = np.maximum(np.where(amax > 0, np.frexp(amax)[1] - 1 + 127, 0) - down, 1)
    scale = np.exp2(byte - 127.0)
    codes = (blocks / scale).astype(np.float32).astype(dtype).astype(np.float64)
    return np.moveaxis((codes * scale).reshape(v.shape), -1, axis)


WIDE = False


def mx_kscale(k):
    if not WIDE:
        return np.ones(k)
    levels = np.array([10, -10, 5, -5, 0])
    if k % 512:
        return np.exp2(np.random.permutation(np.resize(levels, k // 32))).repeat(32)
    a = np.empty((k // 512, 16))
    for p in range(k // 512):
        a[p, :8] = np.random.permutation(np.resize(levels, 8))
        for g in range(8):
            far = levels[np.abs(levels - a[p, g]) >= 10]
            a[p, g + 8] = far[np.random.randint(len(far))]
    return np.exp2(a.ravel()).repeat(32)


def f64(x):
    return np.asarray(x).astype(np.float64)


def striped(idx):
    return np.tile(np.asarray(idx).reshape(-1, 16).T, (8, 1)).astype(np.uint16)


def unstriped(offs):
    return offs[:16].T.reshape(-1).astype(np.int64)


def striped8(idx):
    return np.asarray(idx).reshape(8, -1, 16).transpose(0, 2, 1).reshape(128, -1).astype(np.uint16)


def unstriped8(offs):
    return offs.reshape(8, 16, -1).transpose(0, 2, 1).reshape(8, -1).astype(np.int64)


def pick8(x, idx, run):
    r = np.arange(len(x))
    return x[r[:, None], idx[r % (8 * run) // run]]


E2M1 = np.array([0.0, 0.5, 1.0, 1.5, 2.0, 3.0, 4.0, 6.0, -0.0, -0.5, -1.0, -1.5, -2.0, -3.0, -4.0, -6.0])


def pack_weight(w, fmt):
    k, n = w.shape
    w = f64(np.asarray(w, np.float32).astype(ml_dtypes.bfloat16)).reshape(k // 32, 32, n)
    amax = np.abs(w).max(1)
    if fmt == "e4m3":
        byte = np.frexp(amax)[1] - 1 + 127 - 7
    else:
        mant, ex = np.frexp(amax / 6.0)
        byte = np.where(mant > 0.5, ex, ex - 1) + 127
    byte = np.clip(np.where(amax > 0, byte, 1), 1, 254)
    scaled = (w * np.exp2(127.0 - byte)[:, None, :]).reshape(k, n).astype(np.float32)
    by_word = np.ascontiguousarray(scaled.reshape(k // 512, 128, 4, n).transpose(0, 1, 3, 2))
    if fmt == "e4m3":
        words = by_word.astype(ml_dtypes.float8_e4m3fn).view(np.uint8)
    else:
        c = by_word.astype(ml_dtypes.float4_e2m1fn).view(np.uint8) & 0xF
        words = (c[..., 0::2] | (c[..., 1::2] << 4)).reshape(k // 512, 128, 2 * n)
    return np.ascontiguousarray(words), np.ascontiguousarray(byte.astype(np.uint8).reshape(k // 512, 16, n))


def unpack_weight(words, scales, fmt):
    g, _, n = scales.shape
    words = np.ascontiguousarray(words).reshape(g, 128, n, -1)
    if fmt == "e4m3":
        vals = words.view(ml_dtypes.float8_e4m3fn).astype(np.float64)
    else:
        nib = np.empty((g, 128, n, 4), np.uint8)
        nib[..., 0::2] = words & 0xF
        nib[..., 1::2] = words >> 4
        vals = E2M1[nib]
    vals = vals * np.repeat(np.exp2(scales.astype(np.float64) - 127.0), 8, axis=1)[..., None]
    return vals.transpose(0, 1, 3, 2).reshape(g * 512, n)


K, J, R, T, F, C, O, N, U = 512, 512, 512, 1024, 1024, 1024, 512, 256, 1024


def setup_inputs():
    n = np.random.standard_normal
    idx = np.random.permutation(T)[:J]
    idx2 = np.random.permutation(F)[:R]
    idx3 = np.stack([np.random.permutation(C)[:J] for _ in range(8)])
    idx4 = np.stack([np.random.permutation(C)[:J] for _ in range(8)])
    idx5 = np.stack([np.random.permutation(C)[:O] for _ in range(8)])
    idx6 = np.stack([np.random.permutation(U)[:O] for _ in range(8)])
    idx7 = np.stack([np.random.permutation(U)[:O] for _ in range(8)])
    fk = mx_kscale(K)
    fr = mx_kscale(R)
    tr = np.ones(F)
    tr[idx2] = fr
    xtp = pack_weight(n((K, T)) * fk[:, None], "e4m3")
    wtp = pack_weight(n((K, F)) * 1 / np.sqrt(K) / fk[:, None] * tr, "e2m1")
    wbp = pack_weight(n((R, N)) * 1 / np.sqrt(R) / fr[:, None], "e4m3")
    return {
        "xt_words": xtp[0],
        "xt_scales": xtp[1],
        "wt_words": wtp[0],
        "wt_scales": wtp[1],
        "sa": (np.random.uniform(0.5, 1.6, (R, 1))).astype(np.float32),
        "wb_words": wbp[0],
        "wb_scales": wbp[1],
        "offs": striped(idx),
        "offs2": striped(idx2),
        "offs3": striped8(idx3),
        "offs4": striped8(idx4),
        "offs5": striped8(idx5),
        "offs6": striped8(idx6),
        "offs7": striped8(idx7),
    }


def reference(xt_words, xt_scales, wt_words, wt_scales, sa, wb_words, wb_scales, offs, offs2, offs3, offs4, offs5, offs6, offs7):
    idx = unstriped(offs)
    idx2 = unstriped(offs2)
    idx3 = unstriped8(offs3)
    idx4 = unstriped8(offs4)
    idx5 = unstriped8(offs5)
    idx6 = unstriped8(offs6)
    idx7 = unstriped8(offs7)
    xtu = unpack_weight(xt_words, xt_scales, "e4m3")
    wtu = unpack_weight(wt_words, wt_scales, "e2m1")
    wbu = unpack_weight(wb_words, wb_scales, "e4m3")
    wtidx2g = wtu[:, idx2]
    xtidxg = xtu[:, idx]
    a = wtidx2g.T @ xtidxg
    pw = np.zeros((R, C))
    pw[np.arange(R)[:, None], idx3[np.arange(R) % 512 // 64]] = a
    pv = np.zeros((R, C))
    pv[np.arange(R)[:, None], idx4[np.arange(R) % 512 // 64]] = a
    ph = np.maximum(pw, pv)
    g1 = np.pad(ph, ((0, 0), (1, 0)))[:, :C]
    g2 = np.pad(ph, ((0, 0), (2, 0)))[:, :C]
    pg = np.abs(ph - g1 * 2.0 + g2)
    hid = pick8(pg, idx5, 64) * f64(sa)
    hidq = mxq(hid, 0, "e4m3")
    p = wbu.T @ hidq
    m0 = np.maximum(p, 0.0)
    m1 = np.maximum(-p, 0.0)
    m2 = np.zeros((N, U))
    m2[np.arange(N)[:, None], idx6[np.arange(N) % 128 // 16]] = m0
    m3 = np.zeros((N, U))
    m3[np.arange(N)[:, None], idx7[np.arange(N) % 128 // 16]] = m1
    y = m2 - m3
    return y

@@ -1,0 +1,237 @@
+from contextlib import ExitStack
+
+import concourse.mybir as mybir
+
+K, J, R, T, F, C, O, N, U = 512, 512, 512, 1024, 1024, 1024, 512, 256, 1024
+FLOPS = 2 * K * R * J + 2 * R * N * O
+
+F32 = mybir.dt.float32
+BF16 = mybir.dt.bfloat16
+I32 = mybir.dt.int32
+U32 = mybir.dt.uint32
+U16 = mybir.dt.uint16
+U8 = mybir.dt.uint8
+E4M3 = mybir.dt.float8_e4m3fn_x4
+E2M1 = mybir.dt.float4_e2m1fn_x4
+ALU = mybir.AluOpType
+COPY = mybir.ActivationFunctionType.Copy
+
+P = 128
+PACK = 4
+STRIPE = 16
+LEAD = 128
+PAD = 4
+
+
+def entries(offsets, lo, hi):
+    return offsets[:, lo // STRIPE : hi // STRIPE]
+
+
+def load_scale_rows(queue, plane, rows):
+    for q in range(4):
+        queue.dma_start(out=plane[32 * q : 32 * q + 4, :].bitcast(I32), in_=rows[4 * q : 4 * q + 4, :].bitcast(I32))
+
+
+def tile_picked_tokens_store_one_curvature_one_endsplit_kernel(
+    tc, xt_words, xt_scales, wt_words, wt_scales, sa, wb_words, wb_scales,
+    offs, offs2, offs3, offs4, offs5, offs6, offs7, out,
+):
+    nc = tc.nc
+    with ExitStack() as ctx:
+        lists = ctx.enter_context(tc.tile_pool(name="lists", bufs=1))
+        keep = ctx.enter_context(tc.tile_pool(name="keep", bufs=1))
+        early = ctx.enter_context(tc.tile_pool(name="early", bufs=1))
+        shared = ctx.enter_context(tc.tile_pool(name="shared", bufs=1))
+        late = ctx.enter_context(tc.tile_pool(name="late", bufs=1))
+        psum = ctx.enter_context(tc.psum_pool(name="psum", bufs=1))
+
+        idx, idx2, idx3, idx4, idx5, idx6, idx7 = [
+            lists.tile([P, J // STRIPE], U16, name="list%d" % i) for i in range(1, 8)
+        ]
+
+        wt_w = keep.tile([P, F], U16, align_bytes=64)
+        wt_s = keep.tile([P, F], U8, align_bytes=64)
+        xt_w = shared.tile([P, T], U32, align_bytes=64, offset=2048)
+        xt_s = shared.tile([P, T], U8, align_bytes=64, offset=12288 + 3072)
+        wb_w = early.tile([P, N], U32, offset=0, align_bytes=64)
+        wb_s = early.tile([P, N], U8, offset=1024, align_bytes=64)
+        sa_t = early.tile([P, PACK], F32, offset=1280)
+
+        for plane in (wt_s, xt_s):
+            nc.vector.memset(plane[:].bitcast(I32), 0)
+
+        nc.sync.dma_start(out=idx2[:], in_=offs2)
+        load_scale_rows(nc.scalar, wt_s, wt_scales[0])
+        nc.sync.dma_start(out=wt_w[:].bitcast(I32), in_=wt_words[0].bitcast(I32))
+        nc.sync.dma_start(out=xt_w[:].bitcast(I32), in_=xt_words[0].rearrange("p c b -> p (c b)").bitcast(I32))
+        nc.sync.dma_start(out=idx[:], in_=offs)
+        load_scale_rows(nc.scalar, xt_s, xt_scales[0])
+        nc.sync.dma_start(out=idx3[:], in_=offs3)
+        nc.sync.dma_start(out=idx4[:], in_=offs4)
+        nc.sync.dma_start(out=idx5[:], in_=offs5)
+        nc.sync.dma_start(out=idx6[:], in_=offs6)
+        nc.sync.dma_start(out=idx7[:], in_=offs7)
+
+        wg_w = early.tile([P, R], U16, align_bytes=64, offset=512)
+        wg_s = keep.tile([P, R], U8, align_bytes=64)
+        lead_w = keep.tile([P, LEAD], U32, align_bytes=64)
+        rest_w = shared.tile([P, J - LEAD], U32, align_bytes=64, offset=12288 + 3072)
+        xg_s = shared.tile([P, J], U8, align_bytes=64, offset=20480 + 3840)
+        first_w = keep.tile([P, 1, 2 * P], U8, align_bytes=64)
+        first_s = keep.tile([P, 1, P], U8, align_bytes=64)
+        other_w = shared.tile([P, PACK - 1, 2 * P], U8, align_bytes=64, offset=3712)
+        other_s = shared.tile([P, PACK - 1, P], U8, align_bytes=64, offset=3072)
+        wd_w = [first_w[:, 0, :]] + [other_w[:, t, :] for t in range(PACK - 1)]
+        wd_s = [first_s[:, 0, :]] + [other_s[:, t, :] for t in range(PACK - 1)]
+
+        def deal(words, scales, lo, hi):
+            nc.vector.tensor_copy(
+                out=words[:].rearrange("p t (m b) -> p t m b", b=2),
+                in_=wg_w[:].bitcast(U8).rearrange("p (m t b) -> p t m b", t=PACK, b=2)[:, lo:hi],
+            )
+            nc.vector.tensor_copy(out=scales[:], in_=wg_s[:].rearrange("p (m t) -> p t m", t=PACK)[:, lo:hi])
+
+        def first_product(bank, t, words, lo, hi):
+            nc.tensor.matmul_mx(
+                out=bank,
+                lhsT=wd_w[t].bitcast(E2M1),
+                lhsT_scale=wd_s[t],
+                rhs=words.bitcast(E4M3),
+                rhs_scale=xg_s[:, lo:hi],
+                start=True,
+                stop=True,
+            )
+
+        def rest_products(bank, t):
+            first_product(bank[:, 0:LEAD], t, rest_w[:, 0:LEAD], LEAD, 2 * LEAD)
+            first_product(bank[:, LEAD:], t, rest_w[:, LEAD:], 2 * LEAD, J)
+
+        nc.vector.tensor_copy(out=wg_s[:], in_=wt_s[:].indirect(idx2[:]))
+        nc.vector.tensor_copy(out=wg_w[:], in_=wt_w[:].indirect(idx2[:]))
+        deal(first_w, first_s, 0, 1)
+        nc.vector.tensor_copy(out=lead_w[:], in_=xt_w[:].indirect(entries(idx, 0, LEAD)))
+        nc.vector.tensor_copy(out=xg_s[:, 0:LEAD], in_=xt_s[:].indirect(entries(idx, 0, LEAD)))
+
+        a = [keep.tile([P, J], F32, name="a%d" % t) for t in range(PACK - 1)]
+        a.append(late.tile([P, J], F32, name="a3", offset=1024))
+
+        lead_bank = psum.tile([P, LEAD], F32, name="lead_bank", tag="bank0")
+        first_product(lead_bank[:], 0, lead_w[:], 0, LEAD)
+        nc.scalar.activation(out=a[0][:, 0:LEAD], in_=lead_bank[:], func=COPY)
+
+        nc.vector.tensor_copy(out=xg_s[:, LEAD:], in_=xt_s[:].indirect(entries(idx, LEAD, J)))
+        nc.vector.tensor_copy(out=rest_w[:], in_=xt_w[:].indirect(entries(idx, LEAD, J)))
+        rest_bank = psum.tile([P, J - LEAD], F32, name="rest_bank", tag="bank1")
+        rest_products(rest_bank[:], 0)
+        nc.vector.tensor_copy(out=a[0][:, LEAD:], in_=rest_bank[:])
+        deal(other_w, other_s, 1, PACK)
+        for t in range(1, PACK):
+            bank = psum.tile([P, J], F32, name="a_bank%d" % t, tag="bank%d" % (t + 1))
+            first_product(bank[:, 0:LEAD], t, lead_w[:], 0, LEAD)
+            rest_products(bank[:, LEAD:], t)
+            nc.vector.tensor_copy(out=a[t][:], in_=bank[:])
+
+        nc.vector.memset(wb_s[:].bitcast(I32), 0)
+        nc.sync.dma_start(out=sa_t[:], in_=sa.rearrange("(p t) o -> p (t o)", t=PACK))
+        nc.sync.dma_start(out=wb_w[:].bitcast(I32), in_=wb_words[0].rearrange("p c b -> p (c b)").bitcast(I32))
+        load_scale_rows(nc.sync, wb_s, wb_scales[0])
+
+        pw = [keep.tile([P, C], F32, name="pw0"), shared.tile([P, C], F32, name="pw1", offset=0)]
+        pv = [keep.tile([P, C], F32, name="pv0"), shared.tile([P, C], F32, name="pv1", offset=4096)]
+        m2 = [shared.tile([P, U], F32, name="m2_%d" % i, offset=12288 + 8192 * i) for i in range(2)]
+        m3 = [shared.tile([P, U], F32, name="m3_%d" % i, offset=16384 + 8192 * i) for i in range(2)]
+        ph = keep.tile([P, PAD + C], F32)
+        nc.vector.memset(ph[:, PAD - 2 : PAD], 0.0)
+        for window in (pw[0], pv[0], pw[1], pv[1], m2[0], m3[0], m2[1], m3[1]):
+            nc.vector.memset(window[:], 0.0)
+
+        def scatter(window, offsets, values, lo, hi):
+            nc.scalar.activation(out=window[:].indirect(entries(offsets, lo, hi)), in_=values, func=COPY)
+
+        ends = keep.tile([P, C], F32)
+        bend = keep.tile([P, C], F32)
+        pg = [keep.tile([P, C], F32, name="pg%d" % t) for t in range(PACK)]
+        halves = [(0, C // 2), (C // 2, C)]
+        for t in range(PACK):
+            w, v = pw[t % 2], pv[t % 2]
+            pieces = [(0, LEAD), (LEAD, J)] if t == 0 else [(0, J)]
+            for lo, hi in pieces:
+                scatter(w, idx3, a[t][:, lo:hi], lo, hi)
+                scatter(v, idx4, a[t][:, lo:hi], lo, hi)
+            for lo, hi in halves:
+                nc.vector.tensor_tensor(out=ph[:, PAD + lo : PAD + hi], in0=w[:, lo:hi], in1=v[:, lo:hi], op=ALU.max)
+            for lo, hi in halves:
+                nc.vector.tensor_tensor(
+                    out=ends[:, lo:hi], in0=ph[:, PAD + lo : PAD + hi], in1=ph[:, PAD - 2 + lo : PAD - 2 + hi], op=ALU.add
+                )
+            for lo, hi in halves:
+                nc.vector.scalar_tensor_tensor(
+                    out=bend[:, lo:hi], in0=ph[:, PAD - 1 + lo : PAD - 1 + hi], scalar=-2.0, in1=ends[:, lo:hi],
+                    op0=ALU.mult, op1=ALU.add,
+                )
+            for lo, hi in halves:
+                nc.vector.scalar_tensor_tensor(
+                    out=pg[t][:, lo:hi], in0=bend[:, lo:hi], scalar=-1.0, in1=bend[:, lo:hi], op0=ALU.mult, op1=ALU.max
+                )
+
+        HALF = O // 2
+        hid = [late.tile([P, PACK, HALF], BF16, name="hid%d" % h, offset=2048 * h) for h in range(2)]
+
+        def fetch(t, h):
+            nc.scalar.activation(
+                out=hid[h][:, t, :], in_=pg[t][:].indirect(entries(idx5, h * HALF, (h + 1) * HALF)),
+                func=COPY, scale=sa_t[:, t : t + 1],
+            )
+
+        for h in range(2):
+            for t in range(PACK - 1):
+                fetch(t, h)
+        fetch(PACK - 1, 0)
+        fetch(PACK - 1, 1)
+
+        def weave(dst, src):
+            nc.vector.tensor_copy(
+                out=dst.rearrange("p (c i t) -> p c t i", i=4, t=PACK),
+                in_=src.rearrange("p t (c i) -> p c t i", i=4),
+            )
+
+        m0 = [keep.tile([P, O], F32, name="m0_%d" % i) for i in range(2)]
+        m1 = [keep.tile([P, O], F32, name="m1_%d" % i) for i in range(2)]
+
+        def second_product(bank, i, codes, scales):
+            nc.tensor.matmul_mx(
+                out=bank,
+                lhsT=wb_w[:, i * P : (i + 1) * P].bitcast(E4M3),
+                lhsT_scale=wb_s[:, i * P : (i + 1) * P],
+                rhs=codes.bitcast(E4M3),
+                rhs_scale=scales,
+                start=True,
+                stop=True,
+            )
+
+        def split_by_sign(i, bank, lo, hi):
+            nc.vector.tensor_scalar(out=m0[i][:, lo:hi], in0=bank, scalar1=0.0, scalar2=None, op0=ALU.max)
+            nc.vector.tensor_scalar(out=m1[i][:, lo:hi], in0=bank, scalar1=-1.0, scalar2=0.0, op0=ALU.mult, op1=ALU.max)
+
+        stages = [(0, LEAD), (LEAD, HALF), (HALF, O)]
+        for s, (lo, hi) in enumerate(stages):
+            width = hi - lo
+            woven = keep.tile([P, PACK * width], BF16, align_bytes=64, name="woven%d" % s)
+            codes = keep.tile([P, width], U32, align_bytes=64, name="codes%d" % s)
+            scales = keep.tile([P, width], U8, align_bytes=64, name="scales%d" % s)
+            weave(woven[:], hid[lo // HALF][:, :, lo % HALF : lo % HALF + width])
+            nc.vector.quantize_mx(out=codes[:].bitcast(E4M3), scales=scales[:], in_=woven[:])
+            for i in range(2):
+                bank = psum.tile([P, width], F32, name="p%d_%d" % (s, i), tag="bank%d" % (2 * s + i))
+                second_product(bank[:], i, codes[:], scales[:])
+                split_by_sign(i, bank[:], lo, hi)
+            for i in range(2):
+                scatter(m2[i], idx6, m0[i][:, lo:hi], lo, hi)
+                scatter(m3[i], idx7, m1[i][:, lo:hi], lo, hi)
+
+        for i in range(2):
+            y = keep.tile([P, U], F32, name="y%d" % i)
+            for s in range(4):
+                lo, hi = s * U // 4, (s + 1) * U // 4
+                nc.vector.tensor_tensor(out=y[:, lo:hi], in0=m2[i][:, lo:hi], in1=m3[i][:, lo:hi], op=ALU.subtract)
+                nc.sync.dma_start(out=out[i * P : (i + 1) * P, lo:hi], in_=y[:, lo:hi])

@@ -15,12 +15,14 @@ E4M3 = mybir.dt.float8_e4m3fn_x4
 E2M1 = mybir.dt.float4_e2m1fn_x4
 ALU = mybir.AluOpType
 COPY = mybir.ActivationFunctionType.Copy
+ABS = mybir.ActivationFunctionType.Abs
 
 P = 128
 PACK = 4
 STRIPE = 16
 LEAD = 128
 PAD = 4
+SPLIT = 512
 
 
 def entries(offsets, lo, hi):
@@ -51,7 +53,7 @@ def tile_picked_tokens_store_one_curvature_one_endsplit_kernel(
 
         wt_w = keep.tile([P, F], U16, align_bytes=64)
         wt_s = keep.tile([P, F], U8, align_bytes=64)
-        xt_w = shared.tile([P, T], U32, align_bytes=64, offset=2048)
+        xt_w = keep.tile([P, T], U32, align_bytes=64)
         xt_s = shared.tile([P, T], U8, align_bytes=64, offset=12288 + 3072)
         wb_w = early.tile([P, N], U32, offset=0, align_bytes=64)
         wb_s = early.tile([P, N], U8, offset=1024, align_bytes=64)
@@ -60,12 +62,12 @@ def tile_picked_tokens_store_one_curvature_one_endsplit_kernel(
         for plane in (wt_s, xt_s):
             nc.vector.memset(plane[:].bitcast(I32), 0)
 
-        nc.sync.dma_start(out=idx2[:], in_=offs2)
-        load_scale_rows(nc.scalar, wt_s, wt_scales[0])
         nc.sync.dma_start(out=wt_w[:].bitcast(I32), in_=wt_words[0].bitcast(I32))
+        nc.sync.dma_start(out=idx2[:], in_=offs2)
+        load_scale_rows(nc.sync, wt_s, wt_scales[0])
         nc.sync.dma_start(out=xt_w[:].bitcast(I32), in_=xt_words[0].rearrange("p c b -> p (c b)").bitcast(I32))
         nc.sync.dma_start(out=idx[:], in_=offs)
-        load_scale_rows(nc.scalar, xt_s, xt_scales[0])
+        load_scale_rows(nc.sync, xt_s, xt_scales[0])
         nc.sync.dma_start(out=idx3[:], in_=offs3)
         nc.sync.dma_start(out=idx4[:], in_=offs4)
         nc.sync.dma_start(out=idx5[:], in_=offs5)
@@ -77,10 +79,10 @@ def tile_picked_tokens_store_one_curvature_one_endsplit_kernel(
         lead_w = keep.tile([P, LEAD], U32, align_bytes=64)
         rest_w = shared.tile([P, J - LEAD], U32, align_bytes=64, offset=12288 + 3072)
         xg_s = shared.tile([P, J], U8, align_bytes=64, offset=20480 + 3840)
-        first_w = keep.tile([P, 1, 2 * P], U8, align_bytes=64)
-        first_s = keep.tile([P, 1, P], U8, align_bytes=64)
-        other_w = shared.tile([P, PACK - 1, 2 * P], U8, align_bytes=64, offset=3712)
-        other_s = shared.tile([P, PACK - 1, P], U8, align_bytes=64, offset=3072)
+        first_w = shared.tile([P, 1, 2 * P], U8, align_bytes=64, offset=4736)
+        first_s = shared.tile([P, 1, P], U8, align_bytes=64, offset=0)
+        other_w = shared.tile([P, PACK - 1, 2 * P], U8, align_bytes=64, offset=4096)
+        other_s = shared.tile([P, PACK - 1, P], U8, align_bytes=64, offset=4864)
         wd_w = [first_w[:, 0, :]] + [other_w[:, t, :] for t in range(PACK - 1)]
         wd_s = [first_s[:, 0, :]] + [other_s[:, t, :] for t in range(PACK - 1)]
 
@@ -106,8 +108,8 @@ def tile_picked_tokens_store_one_curvature_one_endsplit_kernel(
             first_product(bank[:, 0:LEAD], t, rest_w[:, 0:LEAD], LEAD, 2 * LEAD)
             first_product(bank[:, LEAD:], t, rest_w[:, LEAD:], 2 * LEAD, J)
 
-        nc.vector.tensor_copy(out=wg_s[:], in_=wt_s[:].indirect(idx2[:]))
         nc.vector.tensor_copy(out=wg_w[:], in_=wt_w[:].indirect(idx2[:]))
+        nc.vector.tensor_copy(out=wg_s[:], in_=wt_s[:].indirect(idx2[:]))
         deal(first_w, first_s, 0, 1)
         nc.vector.tensor_copy(out=lead_w[:], in_=xt_w[:].indirect(entries(idx, 0, LEAD)))
         nc.vector.tensor_copy(out=xg_s[:, 0:LEAD], in_=xt_s[:].indirect(entries(idx, 0, LEAD)))
@@ -120,13 +122,15 @@ def tile_picked_tokens_store_one_curvature_one_endsplit_kernel(
         nc.scalar.activation(out=a[0][:, 0:LEAD], in_=lead_bank[:], func=COPY)
 
         nc.vector.tensor_copy(out=xg_s[:, LEAD:], in_=xt_s[:].indirect(entries(idx, LEAD, J)))
-        nc.vector.tensor_copy(out=rest_w[:], in_=xt_w[:].indirect(entries(idx, LEAD, J)))
-        rest_bank = psum.tile([P, J - LEAD], F32, name="rest_bank", tag="bank1")
-        rest_products(rest_bank[:], 0)
-        nc.vector.tensor_copy(out=a[0][:, LEAD:], in_=rest_bank[:])
+        for s, (lo, hi) in enumerate(((LEAD, 2 * LEAD), (2 * LEAD, J))):
+            words = rest_w[:, lo - LEAD : hi - LEAD]
+            nc.vector.tensor_copy(out=words, in_=xt_w[:].indirect(entries(idx, lo, hi)))
+            bank = psum.tile([P, hi - lo], F32, name="rest_bank%d" % s, tag="bank%d" % (1 + s))
+            first_product(bank[:], 0, words, lo, hi)
+            nc.vector.tensor_copy(out=a[0][:, lo:hi], in_=bank[:])
         deal(other_w, other_s, 1, PACK)
         for t in range(1, PACK):
-            bank = psum.tile([P, J], F32, name="a_bank%d" % t, tag="bank%d" % (t + 1))
+            bank = psum.tile([P, J], F32, name="a_bank%d" % t, tag="bank%d" % (t + 2))
             first_product(bank[:, 0:LEAD], t, lead_w[:], 0, LEAD)
             rest_products(bank[:, LEAD:], t)
             nc.vector.tensor_copy(out=a[t][:], in_=bank[:])
@@ -151,10 +155,10 @@ def tile_picked_tokens_store_one_curvature_one_endsplit_kernel(
         ends = keep.tile([P, C], F32)
         bend = keep.tile([P, C], F32)
         pg = [keep.tile([P, C], F32, name="pg%d" % t) for t in range(PACK)]
-        halves = [(0, C // 2), (C // 2, C)]
+        halves = [(0, SPLIT), (SPLIT, C)]
         for t in range(PACK):
             w, v = pw[t % 2], pv[t % 2]
-            pieces = [(0, LEAD), (LEAD, J)] if t == 0 else [(0, J)]
+            pieces = [(0, LEAD), (LEAD, 2 * LEAD), (2 * LEAD, J)] if t == 0 else [(0, J)]
             for lo, hi in pieces:
                 scatter(w, idx3, a[t][:, lo:hi], lo, hi)
                 scatter(v, idx4, a[t][:, lo:hi], lo, hi)
@@ -170,9 +174,12 @@ def tile_picked_tokens_store_one_curvature_one_endsplit_kernel(
                     op0=ALU.mult, op1=ALU.add,
                 )
             for lo, hi in halves:
-                nc.vector.scalar_tensor_tensor(
-                    out=pg[t][:, lo:hi], in0=bend[:, lo:hi], scalar=-1.0, in1=bend[:, lo:hi], op0=ALU.mult, op1=ALU.max
-                )
+                if t == PACK - 1 and lo == SPLIT:
+                    nc.scalar.activation(out=pg[t][:, lo:hi], in_=bend[:, lo:hi], func=ABS)
+                else:
+                    nc.vector.scalar_tensor_tensor(
+                        out=pg[t][:, lo:hi], in0=bend[:, lo:hi], scalar=-1.0, in1=bend[:, lo:hi], op0=ALU.mult, op1=ALU.max
+                    )
 
         HALF = O // 2
         hid = [late.tile([P, PACK, HALF], BF16, name="hid%d" % h, offset=2048 * h) for h in range(2)]

@@ -15,6 +15,7 @@ E4M3 = mybir.dt.float8_e4m3fn_x4
 E2M1 = mybir.dt.float4_e2m1fn_x4
 ALU = mybir.AluOpType
 COPY = mybir.ActivationFunctionType.Copy
+RELU = mybir.ActivationFunctionType.Relu
 ABS = mybir.ActivationFunctionType.Abs
 
 P = 128
@@ -22,7 +23,7 @@ PACK = 4
 STRIPE = 16
 LEAD = 128
 PAD = 4
-SPLIT = 512
+SPLIT = 768
 
 
 def entries(offsets, lo, hi):
@@ -153,7 +154,7 @@ def tile_picked_tokens_store_one_curvature_one_endsplit_kernel(
             nc.scalar.activation(out=window[:].indirect(entries(offsets, lo, hi)), in_=values, func=COPY)
 
         ends = keep.tile([P, C], F32)
-        bend = keep.tile([P, C], F32)
+        bend = late.tile([P, C], F32, offset=4096)
         pg = [keep.tile([P, C], F32, name="pg%d" % t) for t in range(PACK)]
         halves = [(0, SPLIT), (SPLIT, C)]
         for t in range(PACK):
@@ -174,7 +175,7 @@ def tile_picked_tokens_store_one_curvature_one_endsplit_kernel(
                     op0=ALU.mult, op1=ALU.add,
                 )
             for lo, hi in halves:
-                if t == PACK - 1 and lo == SPLIT:
+                if t == PACK - 1 and lo == 0:
                     nc.scalar.activation(out=pg[t][:, lo:hi], in_=bend[:, lo:hi], func=ABS)
                 else:
                     nc.vector.scalar_tensor_tensor(
@@ -182,19 +183,18 @@ def tile_picked_tokens_store_one_curvature_one_endsplit_kernel(
                     )
 
         HALF = O // 2
-        hid = [late.tile([P, PACK, HALF], BF16, name="hid%d" % h, offset=2048 * h) for h in range(2)]
+        hid_a = late.tile([P, PACK, HALF], BF16, offset=0)
+        hid_b = [late.tile([P, 2, HALF], BF16, name="hid_b%d" % u, offset=2048 * (1 + u)) for u in range(2)]
 
         def fetch(t, h):
             nc.scalar.activation(
-                out=hid[h][:, t, :], in_=pg[t][:].indirect(entries(idx5, h * HALF, (h + 1) * HALF)),
+                out=hid_b[t // 2][:, t % 2, :] if h else hid_a[:, t, :],
+                in_=pg[t][:].indirect(entries(idx5, h * HALF, (h + 1) * HALF)),
                 func=COPY, scale=sa_t[:, t : t + 1],
             )
 
-        for h in range(2):
-            for t in range(PACK - 1):
-                fetch(t, h)
-        fetch(PACK - 1, 0)
-        fetch(PACK - 1, 1)
+        for t, h in ((0, 0), (1, 0), (2, 0), (0, 1), (1, 1), (3, 0), (2, 1), (3, 1)):
+            fetch(t, h)
 
         def weave(dst, src):
             nc.vector.tensor_copy(
@@ -217,20 +217,36 @@ def tile_picked_tokens_store_one_curvature_one_endsplit_kernel(
             )
 
         def split_by_sign(i, bank, lo, hi):
-            nc.vector.tensor_scalar(out=m0[i][:, lo:hi], in0=bank, scalar1=0.0, scalar2=None, op0=ALU.max)
+            if i == 0 and lo == 0:
+                nc.scalar.activation(out=m0[i][:, lo:hi], in_=bank, func=RELU)
+            else:
+                nc.vector.tensor_scalar(out=m0[i][:, lo:hi], in0=bank, scalar1=0.0, scalar2=None, op0=ALU.max)
             nc.vector.tensor_scalar(out=m1[i][:, lo:hi], in0=bank, scalar1=-1.0, scalar2=0.0, op0=ALU.mult, op1=ALU.max)
 
-        stages = [(0, LEAD), (LEAD, HALF), (HALF, O)]
-        for s, (lo, hi) in enumerate(stages):
+        stages = [[(0, 64)], [(64, LEAD), (LEAD, HALF)], [(HALF, O)]]
+        for s, parts in enumerate(stages):
+            lo, hi = parts[0][0], parts[-1][1]
             width = hi - lo
-            woven = keep.tile([P, PACK * width], BF16, align_bytes=64, name="woven%d" % s)
+            woven = keep.tile([P, PACK * width], BF16, align_bytes=64, name="woven%d" % s, tag="woven")
             codes = keep.tile([P, width], U32, align_bytes=64, name="codes%d" % s)
             scales = keep.tile([P, width], U8, align_bytes=64, name="scales%d" % s)
-            weave(woven[:], hid[lo // HALF][:, :, lo % HALF : lo % HALF + width])
-            nc.vector.quantize_mx(out=codes[:].bitcast(E4M3), scales=scales[:], in_=woven[:])
+            if hi <= HALF:
+                weave(woven[:], hid_a[:, :, lo:hi])
+            else:
+                for u in range(2):
+                    nc.vector.tensor_copy(
+                        out=woven[:].rearrange("p (c u e) -> p c u e", u=2, e=2)[:, :, u, :],
+                        in_=hid_b[u][:].rearrange("p e c -> p c e"),
+                    )
+            for b, e in parts:
+                nc.vector.quantize_mx(
+                    out=codes[:, b - lo : e - lo].bitcast(E4M3), scales=scales[:, b - lo : e - lo],
+                    in_=woven[:, PACK * (b - lo) : PACK * (e - lo)],
+                )
             for i in range(2):
                 bank = psum.tile([P, width], F32, name="p%d_%d" % (s, i), tag="bank%d" % (2 * s + i))
-                second_product(bank[:], i, codes[:], scales[:])
+                for b, e in parts:
+                    second_product(bank[:, b - lo : e - lo], i, codes[:, b - lo : e - lo], scales[:, b - lo : e - lo])
                 split_by_sign(i, bank[:], lo, hi)
             for i in range(2):
                 scatter(m2[i], idx6, m0[i][:, lo:hi], lo, hi)

from contextlib import ExitStack

import concourse.mybir as mybir

K, J, R, T, F, C, O, N, U = 512, 512, 512, 1024, 1024, 1024, 512, 256, 1024
FLOPS = 2 * K * R * J + 2 * R * N * O

F32 = mybir.dt.float32
BF16 = mybir.dt.bfloat16
I32 = mybir.dt.int32
U32 = mybir.dt.uint32
U16 = mybir.dt.uint16
U8 = mybir.dt.uint8
E4M3 = mybir.dt.float8_e4m3fn_x4
E2M1 = mybir.dt.float4_e2m1fn_x4
ALU = mybir.AluOpType
COPY = mybir.ActivationFunctionType.Copy
RELU = mybir.ActivationFunctionType.Relu
ABS = mybir.ActivationFunctionType.Abs

P = 128
PACK = 4
STRIPE = 16
LEAD = 128
PAD = 4
SPLIT = 768


def entries(offsets, lo, hi):
    return offsets[:, lo // STRIPE : hi // STRIPE]


def load_scale_rows(queue, plane, rows):
    for q in range(4):
        queue.dma_start(out=plane[32 * q : 32 * q + 4, :].bitcast(I32), in_=rows[4 * q : 4 * q + 4, :].bitcast(I32))


def tile_picked_tokens_store_one_curvature_one_endsplit_kernel(
    tc, xt_words, xt_scales, wt_words, wt_scales, sa, wb_words, wb_scales,
    offs, offs2, offs3, offs4, offs5, offs6, offs7, out,
):
    nc = tc.nc
    with ExitStack() as ctx:
        lists = ctx.enter_context(tc.tile_pool(name="lists", bufs=1))
        keep = ctx.enter_context(tc.tile_pool(name="keep", bufs=1))
        early = ctx.enter_context(tc.tile_pool(name="early", bufs=1))
        shared = ctx.enter_context(tc.tile_pool(name="shared", bufs=1))
        late = ctx.enter_context(tc.tile_pool(name="late", bufs=1))
        psum = ctx.enter_context(tc.psum_pool(name="psum", bufs=1))

        idx, idx2, idx3, idx4, idx5, idx6, idx7 = [
            lists.tile([P, J // STRIPE], U16, name="list%d" % i) for i in range(1, 8)
        ]

        wt_w = keep.tile([P, F], U16, align_bytes=64)
        wt_s = keep.tile([P, F], U8, align_bytes=64)
        xt_w = keep.tile([P, T], U32, align_bytes=64)
        xt_s = shared.tile([P, T], U8, align_bytes=64, offset=12288 + 3072)
        wb_w = early.tile([P, N], U32, offset=0, align_bytes=64)
        wb_s = early.tile([P, N], U8, offset=1024, align_bytes=64)
        sa_t = early.tile([P, PACK], F32, offset=1280)

        for plane in (wt_s, xt_s):
            nc.vector.memset(plane[:].bitcast(I32), 0)

        nc.sync.dma_start(out=wt_w[:].bitcast(I32), in_=wt_words[0].bitcast(I32))
        nc.sync.dma_start(out=idx2[:], in_=offs2)
        load_scale_rows(nc.sync, wt_s, wt_scales[0])
        nc.sync.dma_start(out=xt_w[:].bitcast(I32), in_=xt_words[0].rearrange("p c b -> p (c b)").bitcast(I32))
        nc.sync.dma_start(out=idx[:], in_=offs)
        load_scale_rows(nc.sync, xt_s, xt_scales[0])
        nc.sync.dma_start(out=idx3[:], in_=offs3)
        nc.sync.dma_start(out=idx4[:], in_=offs4)
        nc.sync.dma_start(out=idx5[:], in_=offs5)
        nc.sync.dma_start(out=idx6[:], in_=offs6)
        nc.sync.dma_start(out=idx7[:], in_=offs7)

        wg_w = early.tile([P, R], U16, align_bytes=64, offset=512)
        wg_s = keep.tile([P, R], U8, align_bytes=64)
        lead_w = keep.tile([P, LEAD], U32, align_bytes=64)
        rest_w = shared.tile([P, J - LEAD], U32, align_bytes=64, offset=12288 + 3072)
        xg_s = shared.tile([P, J], U8, align_bytes=64, offset=20480 + 3840)
        first_w = shared.tile([P, 1, 2 * P], U8, align_bytes=64, offset=4736)
        first_s = shared.tile([P, 1, P], U8, align_bytes=64, offset=0)
        other_w = shared.tile([P, PACK - 1, 2 * P], U8, align_bytes=64, offset=4096)
        other_s = shared.tile([P, PACK - 1, P], U8, align_bytes=64, offset=4864)
        wd_w = [first_w[:, 0, :]] + [other_w[:, t, :] for t in range(PACK - 1)]
        wd_s = [first_s[:, 0, :]] + [other_s[:, t, :] for t in range(PACK - 1)]

        def deal(words, scales, lo, hi):
            nc.vector.tensor_copy(
                out=words[:].rearrange("p t (m b) -> p t m b", b=2),
                in_=wg_w[:].bitcast(U8).rearrange("p (m t b) -> p t m b", t=PACK, b=2)[:, lo:hi],
            )
            nc.vector.tensor_copy(out=scales[:], in_=wg_s[:].rearrange("p (m t) -> p t m", t=PACK)[:, lo:hi])

        def first_product(bank, t, words, lo, hi):
            nc.tensor.matmul_mx(
                out=bank,
                lhsT=wd_w[t].bitcast(E2M1),
                lhsT_scale=wd_s[t],
                rhs=words.bitcast(E4M3),
                rhs_scale=xg_s[:, lo:hi],
                start=True,
                stop=True,
            )

        def rest_products(bank, t):
            first_product(bank[:, 0:LEAD], t, rest_w[:, 0:LEAD], LEAD, 2 * LEAD)
            first_product(bank[:, LEAD:], t, rest_w[:, LEAD:], 2 * LEAD, J)

        nc.vector.tensor_copy(out=wg_w[:], in_=wt_w[:].indirect(idx2[:]))
        nc.vector.tensor_copy(out=wg_s[:], in_=wt_s[:].indirect(idx2[:]))
        deal(first_w, first_s, 0, 1)
        nc.vector.tensor_copy(out=lead_w[:], in_=xt_w[:].indirect(entries(idx, 0, LEAD)))
        nc.vector.tensor_copy(out=xg_s[:, 0:LEAD], in_=xt_s[:].indirect(entries(idx, 0, LEAD)))

        a = [keep.tile([P, J], F32, name="a%d" % t) for t in range(PACK - 1)]
        a.append(late.tile([P, J], F32, name="a3", offset=1024))

        lead_bank = psum.tile([P, LEAD], F32, name="lead_bank", tag="bank0")
        first_product(lead_bank[:], 0, lead_w[:], 0, LEAD)
        nc.scalar.activation(out=a[0][:, 0:LEAD], in_=lead_bank[:], func=COPY)

        nc.vector.tensor_copy(out=xg_s[:, LEAD:], in_=xt_s[:].indirect(entries(idx, LEAD, J)))
        for s, (lo, hi) in enumerate(((LEAD, 2 * LEAD), (2 * LEAD, J))):
            words = rest_w[:, lo - LEAD : hi - LEAD]
            nc.vector.tensor_copy(out=words, in_=xt_w[:].indirect(entries(idx, lo, hi)))
            bank = psum.tile([P, hi - lo], F32, name="rest_bank%d" % s, tag="bank%d" % (1 + s))
            first_product(bank[:], 0, words, lo, hi)
            nc.vector.tensor_copy(out=a[0][:, lo:hi], in_=bank[:])
        deal(other_w, other_s, 1, PACK)
        for t in range(1, PACK):
            bank = psum.tile([P, J], F32, name="a_bank%d" % t, tag="bank%d" % (t + 2))
            first_product(bank[:, 0:LEAD], t, lead_w[:], 0, LEAD)
            rest_products(bank[:, LEAD:], t)
            nc.vector.tensor_copy(out=a[t][:], in_=bank[:])

        nc.vector.memset(wb_s[:].bitcast(I32), 0)
        nc.sync.dma_start(out=sa_t[:], in_=sa.rearrange("(p t) o -> p (t o)", t=PACK))
        nc.sync.dma_start(out=wb_w[:].bitcast(I32), in_=wb_words[0].rearrange("p c b -> p (c b)").bitcast(I32))
        load_scale_rows(nc.sync, wb_s, wb_scales[0])

        pw = [keep.tile([P, C], F32, name="pw0"), shared.tile([P, C], F32, name="pw1", offset=0)]
        pv = [keep.tile([P, C], F32, name="pv0"), shared.tile([P, C], F32, name="pv1", offset=4096)]
        m2 = [shared.tile([P, U], F32, name="m2_%d" % i, offset=12288 + 8192 * i) for i in range(2)]
        m3 = [shared.tile([P, U], F32, name="m3_%d" % i, offset=16384 + 8192 * i) for i in range(2)]
        ph = keep.tile([P, PAD + C], F32)
        nc.vector.memset(ph[:, PAD - 2 : PAD], 0.0)
        for window in (pw[0], pv[0], pw[1], pv[1], m2[0], m3[0], m2[1], m3[1]):
            nc.vector.memset(window[:], 0.0)

        def scatter(window, offsets, values, lo, hi):
            nc.scalar.activation(out=window[:].indirect(entries(offsets, lo, hi)), in_=values, func=COPY)

        ends = keep.tile([P, C], F32)
        bend = late.tile([P, C], F32, offset=4096)
        pg = [keep.tile([P, C], F32, name="pg%d" % t) for t in range(PACK)]
        halves = [(0, SPLIT), (SPLIT, C)]
        for t in range(PACK):
            w, v = pw[t % 2], pv[t % 2]
            pieces = [(0, LEAD), (LEAD, 2 * LEAD), (2 * LEAD, J)] if t == 0 else [(0, J)]
            for lo, hi in pieces:
                scatter(w, idx3, a[t][:, lo:hi], lo, hi)
                scatter(v, idx4, a[t][:, lo:hi], lo, hi)
            for lo, hi in halves:
                nc.vector.tensor_tensor(out=ph[:, PAD + lo : PAD + hi], in0=w[:, lo:hi], in1=v[:, lo:hi], op=ALU.max)
            for lo, hi in halves:
                nc.vector.tensor_tensor(
                    out=ends[:, lo:hi], in0=ph[:, PAD + lo : PAD + hi], in1=ph[:, PAD - 2 + lo : PAD - 2 + hi], op=ALU.add
                )
            for lo, hi in halves:
                nc.vector.scalar_tensor_tensor(
                    out=bend[:, lo:hi], in0=ph[:, PAD - 1 + lo : PAD - 1 + hi], scalar=-2.0, in1=ends[:, lo:hi],
                    op0=ALU.mult, op1=ALU.add,
                )
            for lo, hi in halves:
                if t == PACK - 1 and lo == 0:
                    nc.scalar.activation(out=pg[t][:, lo:hi], in_=bend[:, lo:hi], func=ABS)
                else:
                    nc.vector.scalar_tensor_tensor(
                        out=pg[t][:, lo:hi], in0=bend[:, lo:hi], scalar=-1.0, in1=bend[:, lo:hi], op0=ALU.mult, op1=ALU.max
                    )

        HALF = O // 2
        hid_a = late.tile([P, PACK, HALF], BF16, offset=0)
        hid_b = [late.tile([P, 2, HALF], BF16, name="hid_b%d" % u, offset=2048 * (1 + u)) for u in range(2)]

        def fetch(t, h):
            nc.scalar.activation(
                out=hid_b[t // 2][:, t % 2, :] if h else hid_a[:, t, :],
                in_=pg[t][:].indirect(entries(idx5, h * HALF, (h + 1) * HALF)),
                func=COPY, scale=sa_t[:, t : t + 1],
            )

        for t, h in ((0, 0), (1, 0), (2, 0), (0, 1), (1, 1), (3, 0), (2, 1), (3, 1)):
            fetch(t, h)

        def weave(dst, src):
            nc.vector.tensor_copy(
                out=dst.rearrange("p (c i t) -> p c t i", i=4, t=PACK),
                in_=src.rearrange("p t (c i) -> p c t i", i=4),
            )

        m0 = [keep.tile([P, O], F32, name="m0_%d" % i) for i in range(2)]
        m1 = [keep.tile([P, O], F32, name="m1_%d" % i) for i in range(2)]

        def second_product(bank, i, codes, scales):
            nc.tensor.matmul_mx(
                out=bank,
                lhsT=wb_w[:, i * P : (i + 1) * P].bitcast(E4M3),
                lhsT_scale=wb_s[:, i * P : (i + 1) * P],
                rhs=codes.bitcast(E4M3),
                rhs_scale=scales,
                start=True,
                stop=True,
            )

        def split_by_sign(i, bank, lo, hi):
            if i == 0 and lo == 0:
                nc.scalar.activation(out=m0[i][:, lo:hi], in_=bank, func=RELU)
            else:
                nc.vector.tensor_scalar(out=m0[i][:, lo:hi], in0=bank, scalar1=0.0, scalar2=None, op0=ALU.max)
            nc.vector.tensor_scalar(out=m1[i][:, lo:hi], in0=bank, scalar1=-1.0, scalar2=0.0, op0=ALU.mult, op1=ALU.max)

        stages = [[(0, 64)], [(64, LEAD), (LEAD, HALF)], [(HALF, O)]]
        for s, parts in enumerate(stages):
            lo, hi = parts[0][0], parts[-1][1]
            width = hi - lo
            woven = keep.tile([P, PACK * width], BF16, align_bytes=64, name="woven%d" % s, tag="woven")
            codes = keep.tile([P, width], U32, align_bytes=64, name="codes%d" % s)
            scales = keep.tile([P, width], U8, align_bytes=64, name="scales%d" % s)
            if hi <= HALF:
                weave(woven[:], hid_a[:, :, lo:hi])
            else:
                for u in range(2):
                    nc.vector.tensor_copy(
                        out=woven[:].rearrange("p (c u e) -> p c u e", u=2, e=2)[:, :, u, :],
                        in_=hid_b[u][:].rearrange("p e c -> p c e"),
                    )
            for b, e in parts:
                nc.vector.quantize_mx(
                    out=codes[:, b - lo : e - lo].bitcast(E4M3), scales=scales[:, b - lo : e - lo],
                    in_=woven[:, PACK * (b - lo) : PACK * (e - lo)],
                )
            for i in range(2):
                bank = psum.tile([P, width], F32, name="p%d_%d" % (s, i), tag="bank%d" % (2 * s + i))
                for b, e in parts:
                    second_product(bank[:, b - lo : e - lo], i, codes[:, b - lo : e - lo], scales[:, b - lo : e - lo])
                split_by_sign(i, bank[:], lo, hi)
            for i in range(2):
                scatter(m2[i], idx6, m0[i][:, lo:hi], lo, hi)
                scatter(m3[i], idx7, m1[i][:, lo:hi], lo, hi)

        for i in range(2):
            y = keep.tile([P, U], F32, name="y%d" % i)
            for s in range(4):
                lo, hi = s * U // 4, (s + 1) * U // 4
                nc.vector.tensor_tensor(out=y[:, lo:hi], in0=m2[i][:, lo:hi], in1=m3[i][:, lo:hi], op=ALU.subtract)
                nc.sync.dma_start(out=out[i * P : (i + 1) * P, lo:hi], in_=y[:, lo:hi])
